import numpy as np
import ml_dtypes


def mxq(x, axis, fmt="e4m3"):
    dtype, down = {"e4m3": (ml_dtypes.float8_e4m3fn, 7), "e5m2": (ml_dtypes.float8_e5m2, 14)}[fmt]
    v = np.moveaxis(np.asarray(x, np.float32).astype(ml_dtypes.bfloat16).astype(np.float64), axis, -1)
    blocks = v.reshape(v.shape[:-1] + (-1, 32))
    amax = np.abs(blocks).max(-1, keepdims=True)
    byte = np.maximum(np.where(amax > 0, np.frexp(amax)[1] - 1 + 127, 0) - down, 1)
    scale = np.exp2(byte - 127.0)
    codes = (blocks / scale).astype(np.float32).astype(dtype).astype(np.float64)
    return np.moveaxis((codes * scale).reshape(v.shape), -1, axis)


WIDE = False


def mx_kscale(k):
    if not WIDE:
        return np.ones(k)
    levels = np.array([10, -10, 5, -5, 0])
    if k % 512:
        return np.exp2(np.random.permutation(np.resize(levels, k // 32))).repeat(32)
    a = np.empty((k // 512, 16))
    for p in range(k // 512):
        a[p, :8] = np.random.permutation(np.resize(levels, 8))
        for g in range(8):
            far = levels[np.abs(levels - a[p, g]) >= 10]
            a[p, g + 8] = far[np.random.randint(len(far))]
    return np.exp2(a.ravel()).repeat(32)


BF16 = ml_dtypes.bfloat16


def bf(x):
    return np.asarray(x, np.float32).astype(BF16)


def f64(x):
    return np.asarray(x).astype(np.float64)


E2M1 = np.array([0.0, 0.5, 1.0, 1.5, 2.0, 3.0, 4.0, 6.0, -0.0, -0.5, -1.0, -1.5, -2.0, -3.0, -4.0, -6.0])


def pack_weight(w, fmt):
    k, n = w.shape
    w = f64(bf(w)).reshape(k // 32, 32, n)
    amax = np.abs(w).max(1)
    if fmt == "e4m3":
        byte = np.frexp(amax)[1] - 1 + 127 - 7
    else:
        mant, ex = np.frexp(amax / 6.0)
        byte = np.where(mant > 0.5, ex, ex - 1) + 127
    byte = np.clip(np.where(amax > 0, byte, 1), 1, 254)
    scaled = (w * np.exp2(127.0 - byte)[:, None, :]).reshape(k, n).astype(np.float32)
    by_word = np.ascontiguousarray(scaled.reshape(k // 512, 128, 4, n).transpose(0, 1, 3, 2))
    if fmt == "e4m3":
        words = by_word.astype(ml_dtypes.float8_e4m3fn).view(np.uint8)
    else:
        c = by_word.astype(ml_dtypes.float4_e2m1fn).view(np.uint8) & 0xF
        words = c[..., 0::2] | (c[..., 1::2] << 4)
    return np.ascontiguousarray(words), np.ascontiguousarray(byte.astype(np.uint8).reshape(k // 512, 16, n))


def unpack_weight(words, scales, fmt):
    g, p, n, _ = words.shape
    if fmt == "e4m3":
        vals = np.ascontiguousarray(words).view(ml_dtypes.float8_e4m3fn).astype(np.float64)
    else:
        nib = np.empty((g, p, n, 4), np.uint8)
        nib[..., 0::2] = words & 0xF
        nib[..., 1::2] = words >> 4
        vals = E2M1[nib]
    vals = vals * np.repeat(np.exp2(scales.astype(np.float64) - 127.0), 8, axis=1)[..., None]
    return vals.transpose(0, 1, 3, 2).reshape(g * 512, n)
def pack4(w):
    words, scales = pack_weight(w, "e2m1")
    return words.reshape(words.shape[0], 128, -1), scales


def unpack4(words, scales):
    return unpack_weight(words.reshape(words.shape[0], 128, -1, 2), scales, "e2m1")


M, N, K, L, D = 1024, 1024, 1024, 2048, 1024
GAIN = 1.4


def draw0():
    s, u, t = mx_kscale(K), mx_kscale(L), mx_kscale(D)
    size = GAIN / D ** 0.25
    x = np.random.standard_normal((M, K))
    y = np.random.standard_normal((N, L)) + np.random.standard_normal(L)
    x = x / np.sqrt(np.mean(x ** 2, axis=1, keepdims=True))
    y = y / np.sqrt(np.mean(y ** 2, axis=1, keepdims=True))
    wc = np.random.standard_normal((K, D)) * size / np.sqrt(K)
    wd = np.random.standard_normal((L, D)) * size / np.sqrt(L)
    wd_words, wd_scales = pack4(wd / u[:, None] / t)
    return {"cand": bf(x * s),
            "wc": bf(wc / s[:, None] * t),
            "centre": bf(0.5 * size * np.random.standard_normal(D) * t),
            "corp": bf(y * u),
            "wd_words": wd_words,
            "wd_scales": wd_scales}


def core(cand, wc, centre, corp, wd_words, wd_scales):
    a = (mxq(f64(cand), 1, "e4m3") @ mxq(f64(wc), 0, "e4m3")) - f64(centre)
    b = mxq(f64(corp), 1, "e4m3") @ unpack4(wd_words, wd_scales)
    gram = mxq(a, 1, "e4m3") @ mxq(b, 1, "e4m3").T
    dup = 1.0 / (1.0 + np.exp(-gram))
    density = dup.mean(axis=1)
    return dup, density


def e4m3fn_bytes(y):
    return np.clip(np.asarray(y, np.float64), -448.0, 448.0).astype(np.float32).astype(ml_dtypes.float8_e4m3fn).view(np.uint8)


def e4m3fn_values(b):
    return np.asarray(b, np.uint8).view(ml_dtypes.float8_e4m3fn).astype(np.float64)


def setup_inputs():
    d = draw0()
    x0 = np.asarray(d['corp']).astype(np.float64)
    s = (np.max(np.abs(x0), axis=(0,), keepdims=True) / 448.0).astype(np.float32)
    out = {}
    for k, v in d.items():
        if k == 'corp':
            out['corp_bytes'] = e4m3fn_bytes(x0 / s.astype(np.float64))
            out['corp_scale'] = s
        else:
            out[k] = v
    return out


def reference(cand, wc, centre, corp_bytes, corp_scale, wd_words, wd_scales):
    return core(cand, wc, centre, e4m3fn_values(corp_bytes) * corp_scale.astype(np.float64), wd_words, wd_scales)

from contextlib import ExitStack

import concourse.mybir as mybir
from concourse.masks import make_identity

F32 = mybir.dt.float32
BF16 = mybir.dt.bfloat16
I32 = mybir.dt.int32
U32 = mybir.dt.uint32
U8 = mybir.dt.uint8
CODE = mybir.dt.float8_e4m3fn
E4M3 = mybir.dt.float8_e4m3fn_x4
E2M1 = mybir.dt.float4_e2m1fn_x4
COPY_TABLE = mybir.ActivationFunctionType.Identity
SIGMOID = mybir.ActivationFunctionType.Sigmoid
MULT = mybir.AluOpType.mult
ADD = mybir.AluOpType.add

P = 128
M, N = 1024, 1024
K, L, D = 1024, 2048, 1024
FLOPS = 2 * (M * K * D + N * L * D + M * N * D)


def tile_dedup_density_s11_kernel(
    tc, cand, wc, centre, corp_bytes, corp_scale, wd_words, wd_scales, dup, density
):
    nc = tc.nc
    with ExitStack() as ctx:
        keep = ctx.enter_context(tc.tile_pool(name="keep", bufs=1))
        pool = ctx.enter_context(tc.tile_pool(name="pool", bufs=1))
        psum = ctx.enter_context(tc.psum_pool(name="psum", bufs=8))

        def codes_and_scales(name, shape):
            codes = keep.tile([P] + shape, U32, name=name + "_codes", align_bytes=64)
            scales = keep.tile([P] + shape, U8, name=name + "_scales", align_bytes=64)
            return codes, scales

        cand_mx = [codes_and_scales("cand%d" % h, [2, 512]) for h in range(2)]
        wc_mx = [codes_and_scales("wc%d" % g, [2, 512]) for g in range(2)]
        corp_mx0 = codes_and_scales("corp0", [4, 512])
        corp_mx1 = codes_and_scales("corp1", [2, 2, 512])
        a_mx = [codes_and_scales("a%d" % h, [2, 512]) for h in range(2)]
        b_mx = [codes_and_scales("b%d" % h, [2, 512]) for h in range(2)]
        wd_codes = keep.tile([P, 4, 2 * D], U8, name="wd_codes", align_bytes=64)
        wd_scales_raw = keep.tile([P, 4, D], U8, name="wd_scales_raw", align_bytes=64)
        wd_planes = keep.tile([P, 4, D], U8, name="wd_planes", align_bytes=64)

        identity = keep.tile([P, P], F32, name="identity")
        zeros = keep.tile([P, 512], BF16, name="zeros")
        ones = keep.tile([P, 1], F32, name="ones")
        corp_factor = keep.tile([P, 16], F32, name="corp_factor")
        centre_rows = keep.tile([P, P], BF16, name="centre_rows")
        minus_rows = keep.tile([P, P], F32, name="minus_rows")
        minus_centre = keep.tile([P, 8], F32, name="minus_centre")
        row_sums = keep.tile([P, 2, 8], F32, name="row_sums")
        mean_part = keep.tile([P, 8], F32, name="mean_part")
        mean = keep.tile([P, 8], F32, name="mean")

        def bank(shape):
            return psum.tile(shape, F32, name="bank", tag="bank", bufs=8)

        def grouped(shape):
            return pool.tile(shape, BF16, name="grouped", tag="grouped", bufs=5, align_bytes=64)

        def keep_clock_up(turned, fillers):
            for count in range(fillers):
                out = turned[:].rearrange("p a u n -> p (a u n)")
                nc.tensor.matmul(out, lhsT=zeros[:, 0:P], rhs=zeros[:], start=True, stop=True)

        def quantize(mx, index, values):
            codes, scales = mx
            nc.vector.quantize_mx(out=codes[index].bitcast(E4M3), scales=scales[index], in_=values)

        def vector_copy(out, in_):
            nc.vector.tensor_copy(out=out, in_=in_)

        def scalar_copy(out, in_):
            nc.scalar.copy(out=out, in_=in_)

        cand_raw, corp_raw, wc_raw, wd_raw = {}, {}, {}, {}

        def load_corp_half(i, x):
            tile = pool.tile([P, L // 2], U8, name="corp_half", tag="corp_half", bufs=4)
            nc.sync.dma_start(out=tile[:], in_=corp_bytes[P * i : P * i + P, L // 2 * x : L // 2 * x + L // 2])
            corp_raw[i, x] = tile[:]

        def load_corp(i):
            tile = pool.tile([P, L], U8, name="corp_tile", tag="corp_tile", bufs=5)
            nc.sync.dma_start(out=tile[:], in_=corp_bytes[P * i : P * i + P, :])
            for x in range(2):
                corp_raw[i, x] = tile[:, L // 2 * x : L // 2 * x + L // 2]

        def load_cand(q):
            tile = pool.tile([P, 2, K], BF16, name="cand_pair", tag="cand_pair", bufs=4)
            nc.sync.dma_start(out=tile[:], in_=cand.rearrange("(p j) k -> p j k", j=8)[:, 2 * q : 2 * q + 2, :])
            for j in range(2):
                cand_raw[2 * q + j] = tile[:, j, :]

        def load_wc(k):
            tile = pool.tile([P, 4, D], BF16, name="wc_pass", tag="wc_pass", bufs=2)
            nc.sync.dma_start(out=tile[:], in_=wc.rearrange("(k p t) d -> k p t d", p=P, t=4)[k])
            wc_raw[k] = tile

        def load_wd(q):
            tile = pool.tile([P, 2, 2 * D], U8, name="wd_pair", tag="wd_pair", bufs=2)
            words = wd_words[2 * q : 2 * q + 2].rearrange("g p n -> p g n")
            nc.sync.dma_start(out=tile[:].bitcast(I32), in_=words.bitcast(I32))
            wd_raw[q] = tile

        def load_wd_scales():
            for q in range(4):
                rows = wd_scales[:, 4 * q : 4 * q + 4, :].rearrange("g r n -> r g n")
                nc.sync.dma_start(out=wd_scales_raw[32 * q : 32 * q + 4].bitcast(I32), in_=rows.bitcast(I32))

        def load_corp_scale():
            nc.sync.dma_start(
                out=corp_factor[:].rearrange("p (g t) -> p g t", t=4),
                in_=corp_scale.rearrange("o (g p t) -> p (o g) t", p=P, t=4),
            )

        def load_centre():
            for g in range(2):
                nc.sync.dma_start(
                    out=centre_rows[4 * g : 4 * g + 4, :].rearrange("t (r i) -> t r i", i=4),
                    in_=centre.rearrange("(g r t i) -> g t r i", g=2, t=4, i=4)[g],
                )

        corp_wide, corp_banks, corp_grouped = {}, {}, {}

        def widen(i, x, split):
            tile = pool.tile([P, L // 2], BF16, name="wide", tag="wide", bufs=6)
            codes = corp_raw[i, x].bitcast(CODE)
            if split:
                runs = tile[:].rearrange("p (u w e) -> p w u e", u=2, e=2)
                nc.vector.tensor_scalar(out=runs, in0=codes, scalar1=ones[:], scalar2=None, op0=MULT)
            else:
                nc.scalar.copy(out=tile[:], in_=codes)
            corp_wide[i, x] = tile, split

        def transpose_corp(i, x, fillers=0):
            tile, split = corp_wide[i, x]
            words = tile[:].bitcast(F32)
            turned = bank([P, 2, 2, P])
            keep_clock_up(turned, fillers)
            for g in range(2):
                for u in range(2):
                    start = 256 * u + P * g if split else 256 * g + u
                    step = 1 if split else 2
                    picked = words[:, start : start + step * (P - 1) + 1 : step]
                    nc.tensor.transpose(turned[:, g, u, :], picked, identity[:])
            corp_banks[i, x] = turned

        def scale_corp(i, x):
            h, row = divmod(i, 4)
            if row == 0:
                corp_grouped[h, x] = grouped([P, 2, 512, 4] if h == 0 else [P, 2, 2, 256, 4])
            values = corp_grouped[h, x][:] if h == 0 else corp_grouped[h, x][:, row // 2]
            first = P * row if h == 0 else P * (row % 2)
            for g in range(2):
                column = 4 * (2 * x + g)
                factors = corp_factor[:, column : column + 4].rearrange("p (o u e) -> p o u e", o=1, u=2)
                nc.vector.tensor_tensor(
                    out=values[:, g, first : first + P, :].rearrange("p n (u e) -> p n u e", u=2),
                    in0=corp_banks[i, x][:, g].bitcast(BF16).rearrange("p u (n e) -> p n u e", e=2),
                    in1=factors.to_broadcast([P, P, 2, 2]),
                    op=MULT,
                )

        def quantize_corp_pair(pair):
            for x in range(2):
                values = corp_grouped[1, x][:, pair].rearrange("p g n t -> p (g n t)")
                quantize(corp_mx1, (slice(None), pair, x), values)

        def quantize_corp_half():
            for k in range(4):
                values = corp_grouped[0, k // 2][:, k % 2].rearrange("p n t -> p (n t)")
                quantize(corp_mx0, (slice(None), k), values)

        cand_banks, cand_grouped = {}, {}

        def transpose_cand(j, fillers):
            words = cand_raw[j].bitcast(F32)
            turned = bank([P, 2, 2, P])
            keep_clock_up(turned, fillers)
            for k in range(2):
                for u in range(2):
                    nc.tensor.transpose(turned[:, k, u, :], words[:, 256 * k + u : 256 * (k + 1) : 2], identity[:])
            cand_banks[j] = turned

        def copy_cand(j):
            h, row = divmod(j, 4)
            if row == 0:
                cand_grouped[h] = grouped([P, 2, 512, 4])
            out = cand_grouped[h][:].bitcast(F32)[:, :, P * row : P * row + P, :]
            scalar_copy(out, cand_banks[j][:].rearrange("p k u m -> p k m u"))

        def quantize_cand(h):
            for k in range(2):
                quantize(cand_mx[h], (slice(None), k), cand_grouped[h][:, k].rearrange("p m t -> p (m t)"))

        wc_grouped = {}

        def interleave_wc(k, g):
            wc_grouped[k, g] = pool.tile([P, 512, 4], BF16, name="wc_grouped", tag="wc_grouped", bufs=3, align_bytes=64)
            scalar_copy(
                wc_grouped[k, g][:].rearrange("p (t r i) s -> p t r s i", t=4, i=4),
                wc_raw[k][:, :, 512 * g : 512 * g + 512].rearrange("p s (r t i) -> p t r s i", t=4, i=4),
            )

        def quantize_wc(g):
            for k in range(2):
                quantize(wc_mx[g], (slice(None), k), wc_grouped[k, g][:].rearrange("p c s -> p (c s)"))

        def permute_wd(q):
            two = slice(2 * q, 2 * q + 2)
            vector_copy(
                wd_codes[:, two].rearrange("p g n -> p (g n)").bitcast(I32).rearrange("p (o t r w) -> p o t r w", o=4, t=4, w=2),
                wd_raw[q][:].rearrange("p g n -> p (g n)").bitcast(I32).rearrange("p (o r t w) -> p o t r w", o=4, t=4, w=2),
            )
            vector_copy(
                wd_planes[:, two].rearrange("p g n -> p (g n)").bitcast(I32).rearrange("p (o t r) -> p o t r", o=4, t=4),
                wd_scales_raw[:, two].rearrange("p g n -> p (g n)").bitcast(I32).rearrange("p (o r t) -> p o t r", o=4, t=4),
            )

        def negate_centre():
            nc.vector.tensor_scalar(out=minus_rows[:], in0=centre_rows[:], scalar1=-1.0, scalar2=None, op0=MULT)

        def transpose_centre():
            turned = bank([P, P])
            nc.tensor.transpose(turned[:], minus_rows[:], identity[:])
            return turned

        a_banks, b_banks, g_banks, planes, interleaved = {}, {}, {}, {}, {}

        def wd_stationary(g, t, k):
            column = 512 * g + P * t
            return dict(
                lhsT=wd_codes[:, k, 2 * column : 2 * column + 2 * P].bitcast(E2M1),
                lhsT_scale=wd_planes[:, k, column : column + P],
            )

        def moving(mx, index):
            codes, scales = mx
            return dict(rhs=codes[index].bitcast(E4M3), rhs_scale=scales[index])

        def stationary(mx, index):
            codes, scales = mx
            return dict(lhsT=codes[index].bitcast(E4M3), lhsT_scale=scales[index])

        def multiply_a(h, g):
            for t in range(4):
                out = bank([P, 512])
                for k in range(2):
                    nc.tensor.matmul_mx(
                        out=out[:],
                        **stationary(wc_mx[g], (slice(None), k, slice(P * t, P * t + P))),
                        **moving(cand_mx[h], (slice(None), k)),
                        start=(k == 0),
                        stop=(k == 1),
                    )
                a_banks[h, g, t] = out

        def new_planes():
            return pool.tile([P, 4, 512], BF16, name="planes", tag="planes", bufs=5)

        def subtract_centre(h, g):
            planes["a", h, g] = new_planes()
            for t in range(4):
                nc.scalar.activation(
                    out=planes["a", h, g][:, t, :],
                    in_=a_banks[h, g, t][:],
                    func=COPY_TABLE,
                    bias=minus_centre[:, 4 * g + t : 4 * g + t + 1],
                    scale=1.0,
                )

        def interleave(copy, key):
            interleaved[key] = pool.tile([P, 512, 4], BF16, name="interleaved", tag="interleaved", bufs=3, align_bytes=64)
            copy(
                interleaved[key][:].rearrange("p (c i) t -> p c t i", i=4),
                planes[key][:].rearrange("p t (c i) -> p c t i", i=4),
            )

        def quantize_a(h, g):
            quantize(a_mx[h], (slice(None), g), interleaved["a", h, g][:].rearrange("p m t -> p (m t)"))

        def multiply_b_pair(pair, g):
            for i in range(2):
                out = bank([P, 4, P])
                for t in range(4):
                    for k in range(4):
                        row = 256 * (k % 2) + P * i
                        nc.tensor.matmul_mx(
                            out=out[:, t, :],
                            **wd_stationary(g, t, k),
                            **moving(corp_mx1, (slice(None), pair, k // 2, slice(row, row + P))),
                            start=(k == 0),
                            stop=(k == 3),
                        )
                b_banks["pair", pair, i, g] = out

        def copy_b_pair(copy, pair, g):
            key = "pair", pair, g
            interleaved[key] = pool.tile([P, 512, 4], BF16, name="interleaved", tag="interleaved", bufs=3, align_bytes=64)
            for i in range(2):
                copy(interleaved[key][:, P * i : P * i + P, :], b_banks["pair", pair, i, g][:].rearrange("p t n -> p n t"))

        def quantize_b_pair(pair):
            for g in range(2):
                values = interleaved["pair", pair, g][:, 0:256, :].rearrange("p n t -> p (n t)")
                quantize(b_mx[1], (slice(None), g, slice(256 * pair, 256 * pair + 256)), values)

        def multiply_b(g):
            for t in range(4):
                out = bank([P, 512])
                for k in range(4):
                    nc.tensor.matmul_mx(
                        out=out[:],
                        **wd_stationary(g, t, k),
                        **moving(corp_mx0, (slice(None), k)),
                        start=(k == 0),
                        stop=(k == 3),
                    )
                b_banks["half", g, t] = out

        def copy_b(g):
            planes["b", g] = new_planes()
            for t in range(4):
                scalar_copy(planes["b", g][:, t, :], b_banks["half", g, t][:])

        def quantize_b(g):
            quantize(b_mx[0], (slice(None), g), interleaved["b", g][:].rearrange("p n t -> p (n t)"))

        def similarities(j, h):
            out = bank([P, 512])
            for g in range(2):
                nc.tensor.matmul_mx(
                    out=out[:],
                    **stationary(a_mx[j // 4], (slice(None), g, slice(P * (j % 4), P * (j % 4) + P))),
                    **moving(b_mx[h], (slice(None), g)),
                    start=(g == 0),
                    stop=(g == 1),
                )
            g_banks[j, h] = out

        def sigmoid_and_store(j, h):
            scores = pool.tile([P, 512], F32, name="scores", tag="scores", bufs=5)
            nc.scalar.activation(
                out=scores[:], in_=g_banks[j, h][:], func=SIGMOID, accum_out=row_sums[:, h, j : j + 1]
            )
            nc.sync.dma_start(out=dup.rearrange("(p j) n -> j p n", j=8)[j][:, 512 * h : 512 * h + 512], in_=scores[:])

        nc.vector.memset(zeros[:], 0.0)
        nc.vector.memset(ones[:], 1.0)
        make_identity(nc, identity[:])
        nc.gpsimd.memset(centre_rows[:], 0.0)
        nc.gpsimd.memset(wd_scales_raw[:].bitcast(I32), 0)
        nc.scalar.activation(out=mean_part[:, 0:1], in_=ones[:], func=SIGMOID)

        with tc.manual_schedule():
            for i in range(2):
                for x in range(2):
                    load_corp_half(i, x)
            load_corp_scale()
            load_corp(2)
            load_corp(3)
            load_cand(0)
            load_corp(4)
            load_corp(5)
            for q in range(1, 4):
                load_cand(q)
            load_wd(0)
            load_wd_scales()
            load_wd(1)
            load_wc(0)
            load_centre()
            load_corp(6)
            load_wc(1)
            load_corp(7)

            def turn_corp(i):
                for x in range(2):
                    transpose_corp(i, x, fillers=5 if (i, x) == (0, 0) else 1)
                for x in range(2):
                    scale_corp(i, x)

            def turn_cand(q):
                for j in (2 * q, 2 * q + 1):
                    transpose_cand(j, fillers=1 - j % 2)
                for j in (2 * q, 2 * q + 1):
                    copy_cand(j)

            for i in range(5):
                for x in range(2):
                    widen(i, x, split=(i < 2 and x == 0))
            turn_corp(0)
            turn_corp(1)
            turn_cand(0)
            for x in range(2):
                widen(5, x, split=False)
            turn_corp(2)
            turn_corp(3)
            quantize_corp_half()
            for q in range(1, 4):
                turn_cand(q)
            for q in range(2):
                permute_wd(q)
            quantize_cand(0)
            turn_corp(4)
            turn_corp(5)
            for i in (6, 7):
                for x in range(2):
                    widen(i, x, split=True)
            quantize_corp_pair(0)
            negate_centre()

            for g in range(2):
                multiply_b(g)
            for i in (6, 7):
                for x in range(2):
                    transpose_corp(i, x)
            centre_bank = transpose_centre()
            interleave_wc(0, 0)
            copy_b(0)
            interleave_wc(1, 0)
            copy_b(1)
            interleave_wc(1, 1)
            interleave_wc(0, 1)
            quantize_wc(0)
            vector_copy(minus_centre[:], centre_bank[:, 0:8])
            for i in (6, 7):
                for x in range(2):
                    scale_corp(i, x)
            quantize_cand(1)
            quantize_wc(1)

            for g in range(2):
                multiply_b_pair(0, g)
            for g in range(2):
                for h in range(2):
                    multiply_a(h, g)
            for g in range(2):
                copy_b_pair(scalar_copy, 0, g)
            quantize_b_pair(0)
            quantize_corp_pair(1)
            for g in range(2):
                multiply_b_pair(1, g)
            for g in range(2):
                interleave(vector_copy, ("b", g))
            for g in range(2):
                quantize_b(g)
            for g in range(2):
                for h in range(2):
                    subtract_centre(h, g)
            for g in range(2):
                interleave(vector_copy, ("a", 0, g))
            interleave(scalar_copy, ("a", 1, 1))
            for g in range(2):
                quantize_a(0, g)
            quantize_a(1, 1)
            interleave(vector_copy, ("a", 1, 0))
            quantize_a(1, 0)
            copy_b_pair(scalar_copy, 1, 0)
            copy_b_pair(vector_copy, 1, 1)
            quantize_b_pair(1)

            for h in range(2):
                for j in range(8):
                    similarities(j, h)
                    sigmoid_and_store(j, h)
            nc.vector.tensor_scalar(out=mean_part[:], in0=row_sums[:, 0, :], scalar1=1.0 / N, scalar2=None, op0=MULT)
            nc.vector.scalar_tensor_tensor(
                out=mean[:], in0=row_sums[:, 1, :], scalar=1.0 / N, in1=mean_part[:], op0=MULT, op1=ADD
            )
            nc.sync.dma_start(out=density.rearrange("(p j) -> p j", j=8), in_=mean[:])
